import numpy as np
import ml_dtypes


def mxq(x, axis, fmt="e4m3"):
    dtype, down = {"e4m3": (ml_dtypes.float8_e4m3fn, 7), "e5m2": (ml_dtypes.float8_e5m2, 14)}[fmt]
    v = np.moveaxis(np.asarray(x, np.float32).astype(ml_dtypes.bfloat16).astype(np.float64), axis, -1)
    blocks = v.reshape(v.shape[:-1] + (-1, 32))
    amax = np.abs(blocks).max(-1, keepdims=True)
    byte = np.maximum(np.where(amax > 0, np.frexp(amax)[1] - 1 + 127, 0) - down, 1)
    scale = np.exp2(byte - 127.0)
    codes = (blocks / scale).astype(np.float32).astype(dtype).astype(np.float64)
    return np.moveaxis((codes * scale).reshape(v.shape), -1, axis)


WIDE = False


def mx_kscale(k):
    if not WIDE:
        return np.ones(k)
    levels = np.array([10, -10, 5, -5, 0])
    if k % 512:
        return np.exp2(np.random.permutation(np.resize(levels, k // 32))).repeat(32)
    a = np.empty((k // 512, 16))
    for p in range(k // 512):
        a[p, :8] = np.random.permutation(np.resize(levels, 8))
        for g in range(8):
            far = levels[np.abs(levels - a[p, g]) >= 10]
            a[p, g + 8] = far[np.random.randint(len(far))]
    return np.exp2(a.ravel()).repeat(32)


def f64(x):
    return np.asarray(x).astype(np.float64)


def striped(idx):
    return np.tile(np.asarray(idx).reshape(-1, 16).T, (8, 1)).astype(np.uint16)


def unstriped(offs):
    return offs[:16].T.reshape(-1).astype(np.int64)


def striped8(idx):
    return np.asarray(idx).reshape(8, -1, 16).transpose(0, 2, 1).reshape(128, -1).astype(np.uint16)


def unstriped8(offs):
    return offs.reshape(8, 16, -1).transpose(0, 2, 1).reshape(8, -1).astype(np.int64)


def pick8(x, idx, run):
    r = np.arange(len(x))
    return x[r[:, None], idx[r % (8 * run) // run]]


E2M1 = np.array([0.0, 0.5, 1.0, 1.5, 2.0, 3.0, 4.0, 6.0, -0.0, -0.5, -1.0, -1.5, -2.0, -3.0, -4.0, -6.0])


def pack_weight(w, fmt):
    k, n = w.shape
    w = f64(np.asarray(w, np.float32).astype(ml_dtypes.bfloat16)).reshape(k // 32, 32, n)
    amax = np.abs(w).max(1)
    if fmt == "e4m3":
        byte = np.frexp(amax)[1] - 1 + 127 - 7
    else:
        mant, ex = np.frexp(amax / 6.0)
        byte = np.where(mant > 0.5, ex, ex - 1) + 127
    byte = np.clip(np.where(amax > 0, byte, 1), 1, 254)
    scaled = (w * np.exp2(127.0 - byte)[:, None, :]).reshape(k, n).astype(np.float32)
    by_word = np.ascontiguousarray(scaled.reshape(k // 512, 128, 4, n).transpose(0, 1, 3, 2))
    if fmt == "e4m3":
        words = by_word.astype(ml_dtypes.float8_e4m3fn).view(np.uint8)
    else:
        c = by_word.astype(ml_dtypes.float4_e2m1fn).view(np.uint8) & 0xF
        words = (c[..., 0::2] | (c[..., 1::2] << 4)).reshape(k // 512, 128, 2 * n)
    return np.ascontiguousarray(words), np.ascontiguousarray(byte.astype(np.uint8).reshape(k // 512, 16, n))


def unpack_weight(words, scales, fmt):
    g, _, n = scales.shape
    words = np.ascontiguousarray(words).reshape(g, 128, n, -1)
    if fmt == "e4m3":
        vals = words.view(ml_dtypes.float8_e4m3fn).astype(np.float64)
    else:
        nib = np.empty((g, 128, n, 4), np.uint8)
        nib[..., 0::2] = words & 0xF
        nib[..., 1::2] = words >> 4
        vals = E2M1[nib]
    vals = vals * np.repeat(np.exp2(scales.astype(np.float64) - 127.0), 8, axis=1)[..., None]
    return vals.transpose(0, 1, 3, 2).reshape(g * 512, n)


K, J, R, T, Z, M, C, O, N = 512, 512, 512, 1024, 512, 1024, 1024, 512, 256


def setup_inputs():
    n = np.random.standard_normal
    idx = np.random.permutation(T)[:J]
    idx2 = np.random.permutation(M)[:J]
    idx3 = np.stack([np.random.permutation(C)[:J] for _ in range(8)])
    idx4 = np.stack([np.random.permutation(C)[:O] for _ in range(8)])
    idx5 = np.random.permutation(T)[:O]
    fk = mx_kscale(K)
    fr = mx_kscale(R)
    fz = mx_kscale(Z)
    xtp = pack_weight(n((K, T)) * fk[:, None], "e4m3")
    wp = pack_weight(n((K, R)) * 1 / np.sqrt(K) / fk[:, None] * fr, "e2m1")
    xop = pack_weight(n((Z, M)) / fz[:, None], "e2m1")
    w2p = pack_weight(n((Z, R)) * 1 / np.sqrt(Z) * fz[:, None] * fr, "e4m3")
    wbp = pack_weight(n((R, N)) * 1 / np.sqrt(R) / fr[:, None], "e4m3")
    wsp = pack_weight(n((K, N)) * 1 / np.sqrt(K) / fk[:, None], "e2m1")
    return {
        "xt_words": xtp[0],
        "xt_scales": xtp[1],
        "w_words": wp[0],
        "w_scales": wp[1],
        "xo_words": xop[0],
        "xo_scales": xop[1],
        "w2_words": w2p[0],
        "w2_scales": w2p[1],
        "sa": (np.random.uniform(0.5, 1.6, (R, 1))).astype(np.float32),
        "wb_words": wbp[0],
        "wb_scales": wbp[1],
        "ws_words": wsp[0],
        "ws_scales": wsp[1],
        "offs": striped(idx),
        "offs2": striped(idx2),
        "offs3": striped8(idx3),
        "offs4": striped8(idx4),
        "offs5": striped(idx5),
    }


def reference(xt_words, xt_scales, w_words, w_scales, xo_words, xo_scales, w2_words, w2_scales, sa, wb_words, wb_scales, ws_words, ws_scales, offs, offs2, offs3, offs4, offs5):
    idx = unstriped(offs)
    idx2 = unstriped(offs2)
    idx3 = unstriped8(offs3)
    idx4 = unstriped8(offs4)
    idx5 = unstriped(offs5)
    xtu = unpack_weight(xt_words, xt_scales, "e4m3")
    wu = unpack_weight(w_words, w_scales, "e2m1")
    xou = unpack_weight(xo_words, xo_scales, "e2m1")
    w2u = unpack_weight(w2_words, w2_scales, "e4m3")
    wbu = unpack_weight(wb_words, wb_scales, "e4m3")
    wsu = unpack_weight(ws_words, ws_scales, "e2m1")
    xtidxg = xtu[:, idx]
    xoidx2g = xou[:, idx2]
    a = wu.T @ xtidxg + w2u.T @ xoidx2g
    pw = np.zeros((R, C))
    pw[np.arange(R)[:, None], idx3[np.arange(R) % 512 // 64]] = a
    g0 = np.pad(pw, ((0, 0), (1, 0)))[:, :C]
    g1 = np.maximum(pw, g0)
    g2 = np.pad(g1, ((0, 0), (2, 0)))[:, :C]
    g3 = np.maximum(g1, g2)
    pg = g3 - pw
    hid = pick8(pg, idx4, 64) * f64(sa)
    hidq = mxq(hid, 0, "e4m3")
    xtidx5g = xtu[:, idx5]
    y = wbu.T @ hidq + wsu.T @ xtidx5g
    return y

@@ -1,0 +1,249 @@
+from contextlib import ExitStack
+
+import concourse.mybir as mybir
+
+K, J, R, T, Z, M, C, O, N = 512, 512, 512, 1024, 512, 1024, 1024, 512, 256
+FLOPS = 2 * (K * R * J + Z * R * J + R * N * O + K * N * O)
+
+F32 = mybir.dt.float32
+BF16 = mybir.dt.bfloat16
+I32 = mybir.dt.int32
+U32 = mybir.dt.uint32
+U16 = mybir.dt.uint16
+U8 = mybir.dt.uint8
+FP8X4 = mybir.dt.float8_e4m3fn_x4
+FP4X4 = mybir.dt.float4_e2m1fn_x4
+ALU = mybir.AluOpType
+COPY = mybir.ActivationFunctionType.Copy
+
+P = 128
+PACK = 4
+HALF = 256
+LIST_COLS = HALF // 16
+PAD = 4
+BOARDS = 3
+
+
+def tile_picked_tokens_plain_bank_trailingbest_further_plain_kernel(
+    tc, xt_words, xt_scales, w_words, w_scales, xo_words, xo_scales, w2_words, w2_scales, sa,
+    wb_words, wb_scales, ws_words, ws_scales, offs, offs2, offs3, offs4, offs5, out,
+):
+    nc = tc.nc
+    with ExitStack() as ctx:
+        keep = ctx.enter_context(tc.tile_pool(name="keep", bufs=1))
+        shared = ctx.enter_context(tc.tile_pool(name="shared", bufs=1))
+        psum = ctx.enter_context(tc.psum_pool(name="psum", bufs=1))
+
+        def sb(name, shape, dtype):
+            return keep.tile(shape, dtype, name=name, align_bytes=64)
+
+        def load_list(name, src):
+            t = keep.tile([P, J // 16], U16, name=name)
+            nc.sync.dma_start(t[:], src)
+            return t
+
+        def load_e4m3(name, src):
+            t = sb(name, [P, src.shape[2]], U32)
+            nc.sync.dma_start(t[:].bitcast(I32), src[0].rearrange("p n t -> p (n t)").bitcast(I32))
+            return t
+
+        def load_e2m1(name, src):
+            t = sb(name, [P, src.shape[2] // 2], U16)
+            nc.sync.dma_start(t[:].bitcast(I32), src[0].bitcast(I32))
+            return t
+
+        def cleared_scales(name, src):
+            t = sb(name, [P, src.shape[2]], U8)
+            nc.gpsimd.memset(t[:].bitcast(I32), 0)
+            return t
+
+        def load_scales(queue, t, src):
+            for q in range(4):
+                queue.dma_start(t[32 * q : 32 * q + 4, :].bitcast(I32), src[0, 4 * q : 4 * q + 4, :].bitcast(I32))
+
+        def half(lst, h):
+            return lst[:, h * LIST_COLS : (h + 1) * LIST_COLS]
+
+        xt_s = cleared_scales("xt_s", xt_scales)
+        xo_s = cleared_scales("xo_s", xo_scales)
+        w_st = sb("w_st", [P, 4 * R], U8)
+        w2_st = shared.tile([P, 4 * R], U8, name="w2_st", offset=0, align_bytes=64)
+        for st in (w_st, w2_st):
+            nc.gpsimd.memset(st[:, 0:R].bitcast(I32), 0)
+
+        def load_stage(st, src):
+            nc.sync.dma_start(
+                st[0:4, :].bitcast(I32).rearrange("i (q c) -> i q c", q=4),
+                src[0].bitcast(I32).rearrange("(q i) c -> i q c", q=4),
+            )
+
+        l1 = load_list("l1", offs)
+        load_scales(nc.sync, xt_s, xt_scales)
+        l2 = load_list("l2", offs2)
+        xt_w = load_e4m3("xt_w", xt_words)
+        xo_w = load_e2m1("xo_w", xo_words)
+        load_scales(nc.sync, xo_s, xo_scales)
+        load_stage(w_st, w_scales)
+        load_stage(w2_st, w2_scales)
+        w_w = load_e2m1("w_w", w_words)
+        w2_w = load_e4m3("w2_w", w2_words)
+        l3 = load_list("l3", offs3)
+
+        boards = [sb(f"board{b}", [P, C], F32) for b in range(BOARDS)]
+        nc.vector.memset(boards[0][:], 0.0)
+        nc.gpsimd.memset(boards[1][:], 0.0)
+        g1 = sb("g1", [P, PAD + C], F32)
+        nc.vector.memset(g1[:, 0:PAD], 0.0)
+        wb_s = cleared_scales("wb_s", wb_scales)
+        ws_s = cleared_scales("ws_s", ws_scales)
+        nc.gpsimd.memset(boards[2][:], 0.0)
+
+        l5 = load_list("l5", offs5)
+        l4 = load_list("l4", offs4)
+        sa_t = sb("sa_t", [P, PACK], F32)
+        nc.sync.dma_start(sa_t[:], sa.rearrange("(p t) o -> p (t o)", t=PACK))
+        ws_w = load_e2m1("ws_w", ws_words)
+        load_scales(nc.sync, ws_s, ws_scales)
+        wb_w = load_e4m3("wb_w", wb_words)
+        load_scales(nc.sync, wb_s, wb_scales)
+
+        def gather(name, window, offsets, n, dtype, at=None):
+            if at is None:
+                t = sb(name, [P, n], dtype)
+            else:
+                t = shared.tile([P, n], dtype, name=name, offset=at, align_bytes=64)
+            nc.vector.tensor_copy(t[:], window[:].indirect(offsets))
+            return t
+
+        xg_s, xg_w, og_s, og_w = [None, None], [None, None], [None, None], [None, None]
+        xg_s[0] = gather("xg_s0", xt_s, half(l1, 0), HALF, U8)
+        xg_w[0] = gather("xg_w0", xt_w, half(l1, 0), HALF, U32)
+        og_w[0] = gather("og_w0", xo_w, half(l2, 0), HALF, U16)
+        og_s[0] = gather("og_s0", xo_s, half(l2, 0), HALF, U8)
+        xg_s[1] = gather("xg_s1", xt_s, half(l1, 1), HALF, U8)
+
+        def deal(copy, name, src, dtype):
+            first = sb(name + "_first", [P, P], dtype)
+            rest = sb(name + "_rest", [P, (PACK - 1) * P], dtype)
+            by_t = src[:].rearrange("p (m t) -> p m t", t=PACK)
+            return (
+                [first[:]] + [rest[:, (t - 1) * P : t * P] for t in range(1, PACK)],
+                lambda: copy(first[:], by_t[:, :, 0]),
+                lambda: copy(rest[:].rearrange("p (t m) -> p m t", t=PACK - 1), by_t[:, :, 1:PACK]),
+            )
+
+        wd_w, a0, a1 = deal(nc.scalar.copy, "wd_w", w_w, U16)
+        w2d_w, b0, b1 = deal(nc.scalar.copy, "w2d_w", w2_w, U32)
+        for step in (a0, b0, a1, b1):
+            step()
+
+        def spread(st):
+            for q in range(1, 4):
+                nc.vector.tensor_copy(st[32 * q : 32 * q + 4, 0:R].bitcast(I32), st[0:4, q * R : (q + 1) * R].bitcast(I32))
+
+        def deal_scales(name, st):
+            dealt = sb(name, [P, R], U8)
+            nc.vector.tensor_copy(dealt[:].rearrange("p (t m) -> p t m", t=PACK), st[:, 0:R].rearrange("p (m t) -> p t m", t=PACK))
+            return [dealt[:, t * P : (t + 1) * P] for t in range(PACK)]
+
+        spread(w_st)
+        spread(w2_st)
+        wd_s = deal_scales("wd_s", w_st)
+        w2d_s = deal_scales("w2d_s", w2_st)
+        xg_w[1] = gather("xg_w1", xt_w, half(l1, 1), HALF, U32, at=0)
+        og_w[1] = gather("og_w1", xo_w, half(l2, 1), HALF, U16, at=1024)
+        og_s[1] = gather("og_s1", xo_s, half(l2, 1), HALF, U8, at=1536)
+
+        def first_product(acc, t, h):
+            nc.tensor.matmul_mx(
+                out=acc, lhsT=wd_w[t].bitcast(FP4X4), lhsT_scale=wd_s[t],
+                rhs=xg_w[h][:].bitcast(FP8X4), rhs_scale=xg_s[h][:], start=True, stop=False,
+            )
+            nc.tensor.matmul_mx(
+                out=acc, lhsT=w2d_w[t].bitcast(FP8X4), lhsT_scale=w2d_s[t],
+                rhs=og_w[h][:].bitcast(FP4X4), rhs_scale=og_s[h][:], start=False, stop=True,
+            )
+
+        acc0 = [psum.tile([P, HALF], F32, name=f"acc0{h}", tag=f"bank{h}") for h in range(2)]
+        a0_sb = [sb(f"a0{h}", [P, HALF], F32) for h in range(2)]
+        acc = [None] + [psum.tile([P, J], F32, name=f"acc{t}", tag=f"bank{t + 1}") for t in range(1, PACK)]
+        a_sb = [None] + [sb(f"a{t}", [P, J], F32) for t in range(1, PACK)]
+        first_product(acc0[0][:], 0, 0)
+        nc.scalar.copy(a0_sb[0][:], acc0[0][:])
+        for t in range(1, PACK):
+            first_product(acc[t][:, 0:HALF], t, 0)
+        first_product(acc0[1][:], 0, 1)
+        nc.vector.tensor_copy(a0_sb[1][:], acc0[1][:])
+        for t in range(1, PACK):
+            first_product(acc[t][:, HALF:J], t, 1)
+        nc.vector.tensor_copy(a_sb[1][:], acc[1][:])
+
+        x5_s = gather("x5_s", xt_s, l5[:], O, U8)
+        x5_w = [gather("x5_w0", xt_w, half(l5, 0), HALF, U32), None]
+        y = {}
+
+        def short_way(h):
+            for nt in range(2):
+                rows = slice(nt * P, (nt + 1) * P)
+                y[h, nt] = psum.tile([P, HALF], F32, name=f"y{h}{nt}", tag=f"bank{(5 + 2 * h + nt) % 8}")
+                nc.tensor.matmul_mx(
+                    out=y[h, nt][:], lhsT=ws_w[:, rows].bitcast(FP4X4), lhsT_scale=ws_s[:, rows],
+                    rhs=x5_w[h][:].bitcast(FP8X4), rhs_scale=x5_s[:, h * HALF : (h + 1) * HALF], start=True, stop=False,
+                )
+
+        short_way(0)
+        g3 = shared.tile([P, C], F32, name="g3", offset=2048, align_bytes=64)
+        pg = [sb(f"pg{t}", [P, C], F32) for t in range(PACK)]
+        mid = C // 2
+        for t in range(PACK):
+            pw = boards[t % BOARDS]
+            if t == 0:
+                for h in range(2):
+                    nc.scalar.activation(pw[:].indirect(half(l3, h)), a0_sb[h][:], COPY)
+            else:
+                if t > 1:
+                    nc.scalar.copy(a_sb[t][:], acc[t][:])
+                nc.scalar.activation(pw[:].indirect(l3[:]), a_sb[t][:], COPY)
+            nc.vector.tensor_tensor(g1[:, PAD + 1 : PAD + mid], pw[:, 1:mid], pw[:, 0 : mid - 1], ALU.max)
+            nc.vector.tensor_scalar_max(g1[:, PAD : PAD + 1], pw[:, 0:1], 0.0)
+            nc.vector.tensor_tensor(g1[:, PAD + mid : PAD + C], pw[:, mid:C], pw[:, mid - 1 : C - 1], ALU.max)
+            for lo in (0, mid):
+                nc.vector.tensor_tensor(
+                    g3[:, lo : lo + mid], g1[:, PAD + lo : PAD + lo + mid],
+                    g1[:, PAD + lo - 2 : PAD + lo - 2 + mid], ALU.max,
+                )
+            for lo in (0, mid):
+                nc.vector.tensor_tensor(pg[t][:, lo : lo + mid], g3[:, lo : lo + mid], pw[:, lo : lo + mid], ALU.subtract)
+
+        x5_w[1] = gather("x5_w1", xt_w, half(l5, 1), HALF, U32, at=2048 + 4 * C - 4 * HALF)
+        short_way(1)
+
+        hid = [sb(f"hid{h}", [P, PACK, HALF], BF16) for h in range(2)]
+        for t in range(PACK):
+            for h in range(2):
+                nc.scalar.activation(hid[h][:, t, :], pg[t][:].indirect(half(l4, h)), COPY, scale=sa_t[:, t : t + 1])
+
+        out_v = out.rearrange("(nt p) o -> p nt o", p=P)
+        woven = [sb(f"woven{h}", [P, HALF * PACK], BF16) for h in range(2)]
+        for h in range(2):
+            nc.vector.tensor_copy(
+                woven[h][:].rearrange("p (c i t) -> p c t i", i=4, t=PACK),
+                hid[h][:].rearrange("p t (c i) -> p c t i", i=4),
+            )
+        for h in range(2):
+            hq_w = sb(f"hq_w{h}", [P, HALF], U32)
+            hq_s = sb(f"hq_s{h}", [P, HALF], U8)
+            nc.vector.quantize_mx(out=hq_w[:].bitcast(FP8X4), scales=hq_s[:], in_=woven[h][:])
+            y_sb = sb(f"y_sb{h}", [P, 2, HALF], F32)
+            for nt in range(2):
+                rows = slice(nt * P, (nt + 1) * P)
+                nc.tensor.matmul_mx(
+                    out=y[h, nt][:], lhsT=wb_w[:, rows].bitcast(FP8X4), lhsT_scale=wb_s[:, rows],
+                    rhs=hq_w[:].bitcast(FP8X4), rhs_scale=hq_s[:], start=False, stop=True,
+                )
+            nc.scalar.copy(y_sb[:, 0, :], y[h, 0][:])
+            if h == 0:
+                nc.scalar.copy(y_sb[:, 1, :], y[h, 1][:])
+            else:
+                nc.vector.tensor_copy(y_sb[:, 1, :], y[h, 1][:])
+            nc.sync.dma_start(out_v[:, :, h * HALF : (h + 1) * HALF], y_sb[:])

@@ -42,19 +42,19 @@ def tile_picked_tokens_plain_bank_trailingbest_further_plain_kernel(
             nc.sync.dma_start(t[:], src)
             return t
 
-        def load_e4m3(name, src):
+        def load_e4m3(name, src, queue=nc.sync):
             t = sb(name, [P, src.shape[2]], U32)
-            nc.sync.dma_start(t[:].bitcast(I32), src[0].rearrange("p n t -> p (n t)").bitcast(I32))
+            queue.dma_start(t[:].bitcast(I32), src[0].rearrange("p n t -> p (n t)").bitcast(I32))
             return t
 
-        def load_e2m1(name, src):
+        def load_e2m1(name, src, queue=nc.sync):
             t = sb(name, [P, src.shape[2] // 2], U16)
-            nc.sync.dma_start(t[:].bitcast(I32), src[0].bitcast(I32))
+            queue.dma_start(t[:].bitcast(I32), src[0].bitcast(I32))
             return t
 
-        def cleared_scales(name, src):
+        def cleared_scales(name, src, engine=nc.gpsimd):
             t = sb(name, [P, src.shape[2]], U8)
-            nc.gpsimd.memset(t[:].bitcast(I32), 0)
+            engine.memset(t[:].bitcast(I32), 0)
             return t
 
         def load_scales(queue, t, src):
@@ -65,15 +65,16 @@ def tile_picked_tokens_plain_bank_trailingbest_further_plain_kernel(
             return lst[:, h * LIST_COLS : (h + 1) * LIST_COLS]
 
         xt_s = cleared_scales("xt_s", xt_scales)
-        xo_s = cleared_scales("xo_s", xo_scales)
-        w_st = sb("w_st", [P, 4 * R], U8)
-        w2_st = shared.tile([P, 4 * R], U8, name="w2_st", offset=0, align_bytes=64)
-        for st in (w_st, w2_st):
-            nc.gpsimd.memset(st[:, 0:R].bitcast(I32), 0)
+        w2_w = load_e4m3("w2_w", w2_words, nc.gpsimd)
+        w_w = load_e2m1("w_w", w_words, nc.gpsimd)
+        xo_s = cleared_scales("xo_s", xo_scales, nc.vector)
+        stage = shared.tile([4, 4 * 2 * R], U8, name="stage", offset=0, align_bytes=64)
+        both_s = sb("both_s", [P, 2 * R], U8)
+        nc.gpsimd.memset(both_s[:].bitcast(I32), 0)
 
-        def load_stage(st, src):
+        def load_stage(which, src):
             nc.sync.dma_start(
-                st[0:4, :].bitcast(I32).rearrange("i (q c) -> i q c", q=4),
+                stage[:].bitcast(I32).rearrange("i (q w c) -> i q w c", q=4, w=2)[:, :, which, :],
                 src[0].bitcast(I32).rearrange("(q i) c -> i q c", q=4),
             )
 
@@ -83,10 +84,8 @@ def tile_picked_tokens_plain_bank_trailingbest_further_plain_kernel(
         xt_w = load_e4m3("xt_w", xt_words)
         xo_w = load_e2m1("xo_w", xo_words)
         load_scales(nc.sync, xo_s, xo_scales)
-        load_stage(w_st, w_scales)
-        load_stage(w2_st, w2_scales)
-        w_w = load_e2m1("w_w", w_words)
-        w2_w = load_e4m3("w2_w", w2_words)
+        load_stage(0, w_scales)
+        load_stage(1, w2_scales)
         l3 = load_list("l3", offs3)
 
         boards = [sb(f"board{b}", [P, C], F32) for b in range(BOARDS)]
@@ -122,37 +121,26 @@ def tile_picked_tokens_plain_bank_trailingbest_further_plain_kernel(
         og_s[0] = gather("og_s0", xo_s, half(l2, 0), HALF, U8)
         xg_s[1] = gather("xg_s1", xt_s, half(l1, 1), HALF, U8)
 
-        def deal(copy, name, src, dtype):
-            first = sb(name + "_first", [P, P], dtype)
-            rest = sb(name + "_rest", [P, (PACK - 1) * P], dtype)
-            by_t = src[:].rearrange("p (m t) -> p m t", t=PACK)
-            return (
-                [first[:]] + [rest[:, (t - 1) * P : t * P] for t in range(1, PACK)],
-                lambda: copy(first[:], by_t[:, :, 0]),
-                lambda: copy(rest[:].rearrange("p (t m) -> p m t", t=PACK - 1), by_t[:, :, 1:PACK]),
-            )
-
-        wd_w, a0, a1 = deal(nc.scalar.copy, "wd_w", w_w, U16)
-        w2d_w, b0, b1 = deal(nc.scalar.copy, "w2d_w", w2_w, U32)
-        for step in (a0, b0, a1, b1):
-            step()
-
-        def spread(st):
-            for q in range(1, 4):
-                nc.vector.tensor_copy(st[32 * q : 32 * q + 4, 0:R].bitcast(I32), st[0:4, q * R : (q + 1) * R].bitcast(I32))
-
-        def deal_scales(name, st):
-            dealt = sb(name, [P, R], U8)
-            nc.vector.tensor_copy(dealt[:].rearrange("p (t m) -> p t m", t=PACK), st[:, 0:R].rearrange("p (m t) -> p t m", t=PACK))
+        def deal_words(name, src, dtype):
+            dealt = sb(name, [P, R], dtype)
+            nc.scalar.copy(dealt[:].rearrange("p (t m) -> p m t", t=PACK), src[:].rearrange("p (m t) -> p m t", t=PACK))
             return [dealt[:, t * P : (t + 1) * P] for t in range(PACK)]
 
-        spread(w_st)
-        spread(w2_st)
-        wd_s = deal_scales("wd_s", w_st)
-        w2d_s = deal_scales("w2d_s", w2_st)
+        w2d_w = deal_words("w2d_w", w2_w, U32)
+        wd_w = deal_words("wd_w", w_w, U16)
+
+        for q in range(4):
+            nc.vector.tensor_copy(both_s[32 * q : 32 * q + 4, :].bitcast(I32), stage[:, 2 * R * q : 2 * R * (q + 1)].bitcast(I32))
+        first_s = sb("first_s", [P, 2, P], U8)
+        rest_s = sb("rest_s", [P, 2, PACK - 1, P], U8)
+        both_by_t = both_s[:].rearrange("p (w m t) -> p w t m", w=2, t=PACK)
+        nc.vector.tensor_copy(first_s[:], both_by_t[:, :, 0, :])
         xg_w[1] = gather("xg_w1", xt_w, half(l1, 1), HALF, U32, at=0)
         og_w[1] = gather("og_w1", xo_w, half(l2, 1), HALF, U16, at=1024)
         og_s[1] = gather("og_s1", xo_s, half(l2, 1), HALF, U8, at=1536)
+        nc.vector.tensor_copy(rest_s[:], both_by_t[:, :, 1:PACK, :])
+        wd_s = [first_s[:, 0, :]] + [rest_s[:, 0, t - 1, :] for t in range(1, PACK)]
+        w2d_s = [first_s[:, 1, :]] + [rest_s[:, 1, t - 1, :] for t in range(1, PACK)]
 
         def first_product(acc, t, h):
             nc.tensor.matmul_mx(
@@ -170,11 +158,10 @@ def tile_picked_tokens_plain_bank_trailingbest_further_plain_kernel(
         a_sb = [None] + [sb(f"a{t}", [P, J], F32) for t in range(1, PACK)]
         first_product(acc0[0][:], 0, 0)
         nc.scalar.copy(a0_sb[0][:], acc0[0][:])
-        for t in range(1, PACK):
-            first_product(acc[t][:, 0:HALF], t, 0)
         first_product(acc0[1][:], 0, 1)
         nc.vector.tensor_copy(a0_sb[1][:], acc0[1][:])
         for t in range(1, PACK):
+            first_product(acc[t][:, 0:HALF], t, 0)
             first_product(acc[t][:, HALF:J], t, 1)
         nc.vector.tensor_copy(a_sb[1][:], acc[1][:])
 
@@ -192,7 +179,7 @@ def tile_picked_tokens_plain_bank_trailingbest_further_plain_kernel(
                 )
 
         short_way(0)
-        g3 = shared.tile([P, C], F32, name="g3", offset=2048, align_bytes=64)
+        g3 = shared.tile([P, C], F32, name="g3", offset=4096, align_bytes=64)
         pg = [sb(f"pg{t}", [P, C], F32) for t in range(PACK)]
         mid = C // 2
         for t in range(PACK):
@@ -215,7 +202,7 @@ def tile_picked_tokens_plain_bank_trailingbest_further_plain_kernel(
             for lo in (0, mid):
                 nc.vector.tensor_tensor(pg[t][:, lo : lo + mid], g3[:, lo : lo + mid], pw[:, lo : lo + mid], ALU.subtract)
 
-        x5_w[1] = gather("x5_w1", xt_w, half(l5, 1), HALF, U32, at=2048 + 4 * C - 4 * HALF)
+        x5_w[1] = gather("x5_w1", xt_w, half(l5, 1), HALF, U32, at=4096 + 4 * C - 4 * HALF)
         short_way(1)
 
         hid = [sb(f"hid{h}", [P, PACK, HALF], BF16) for h in range(2)]

@@ -164,9 +164,9 @@ def tile_picked_tokens_plain_bank_trailingbest_further_plain_kernel(
             first_product(acc[t][:, 0:HALF], t, 0)
             first_product(acc[t][:, HALF:J], t, 1)
         nc.vector.tensor_copy(a_sb[1][:], acc[1][:])
+        nc.vector.tensor_copy(a_sb[2][:], acc[2][:])
 
         x5_s = gather("x5_s", xt_s, l5[:], O, U8)
-        x5_w = [gather("x5_w0", xt_w, half(l5, 0), HALF, U32), None]
         y = {}
 
         def short_way(h):
@@ -175,10 +175,8 @@ def tile_picked_tokens_plain_bank_trailingbest_further_plain_kernel(
                 y[h, nt] = psum.tile([P, HALF], F32, name=f"y{h}{nt}", tag=f"bank{(5 + 2 * h + nt) % 8}")
                 nc.tensor.matmul_mx(
                     out=y[h, nt][:], lhsT=ws_w[:, rows].bitcast(FP4X4), lhsT_scale=ws_s[:, rows],
-                    rhs=x5_w[h][:].bitcast(FP8X4), rhs_scale=x5_s[:, h * HALF : (h + 1) * HALF], start=True, stop=False,
+                    rhs=x5_w[:, h * HALF : (h + 1) * HALF].bitcast(FP8X4), rhs_scale=x5_s[:, h * HALF : (h + 1) * HALF], start=True, stop=False,
                 )
-
-        short_way(0)
         g3 = shared.tile([P, C], F32, name="g3", offset=4096, align_bytes=64)
         pg = [sb(f"pg{t}", [P, C], F32) for t in range(PACK)]
         mid = C // 2
@@ -188,7 +186,7 @@ def tile_picked_tokens_plain_bank_trailingbest_further_plain_kernel(
                 for h in range(2):
                     nc.scalar.activation(pw[:].indirect(half(l3, h)), a0_sb[h][:], COPY)
             else:
-                if t > 1:
+                if t > 2:
                     nc.scalar.copy(a_sb[t][:], acc[t][:])
                 nc.scalar.activation(pw[:].indirect(l3[:]), a_sb[t][:], COPY)
             nc.vector.tensor_tensor(g1[:, PAD + 1 : PAD + mid], pw[:, 1:mid], pw[:, 0 : mid - 1], ALU.max)
@@ -202,7 +200,8 @@ def tile_picked_tokens_plain_bank_trailingbest_further_plain_kernel(
             for lo in (0, mid):
                 nc.vector.tensor_tensor(pg[t][:, lo : lo + mid], g3[:, lo : lo + mid], pw[:, lo : lo + mid], ALU.subtract)
 
-        x5_w[1] = gather("x5_w1", xt_w, half(l5, 1), HALF, U32, at=4096 + 4 * C - 4 * HALF)
+        x5_w = gather("x5_w", xt_w, l5[:], O, U32, at=4096 + 4 * C - 4 * O)
+        short_way(0)
         short_way(1)
 
         hid = [sb(f"hid{h}", [P, PACK, HALF], BF16) for h in range(2)]
@@ -210,27 +209,40 @@ def tile_picked_tokens_plain_bank_trailingbest_further_plain_kernel(
             for h in range(2):
                 nc.scalar.activation(hid[h][:, t, :], pg[t][:].indirect(half(l4, h)), COPY, scale=sa_t[:, t : t + 1])
 
-        out_v = out.rearrange("(nt p) o -> p nt o", p=P)
         woven = [sb(f"woven{h}", [P, HALF * PACK], BF16) for h in range(2)]
-        for h in range(2):
+
+        def weave(h, lo, hi):
             nc.vector.tensor_copy(
-                woven[h][:].rearrange("p (c i t) -> p c t i", i=4, t=PACK),
-                hid[h][:].rearrange("p t (c i) -> p c t i", i=4),
+                woven[h][:, PACK * lo : PACK * hi].rearrange("p (c i t) -> p c t i", i=4, t=PACK),
+                hid[h][:, :, lo:hi].rearrange("p t (c i) -> p c t i", i=4),
             )
+
+        weave(0, 0, HALF)
+        weave(1, 0, P)
+        nc.scalar.copy(
+            woven[1][:, PACK * P : PACK * HALF].rearrange("p (c t) -> p c t", t=PACK),
+            hid[1][:, :, P:HALF].rearrange("p t c -> p c t"),
+        )
         for h in range(2):
             hq_w = sb(f"hq_w{h}", [P, HALF], U32)
             hq_s = sb(f"hq_s{h}", [P, HALF], U8)
             nc.vector.quantize_mx(out=hq_w[:].bitcast(FP8X4), scales=hq_s[:], in_=woven[h][:])
-            y_sb = sb(f"y_sb{h}", [P, 2, HALF], F32)
             for nt in range(2):
                 rows = slice(nt * P, (nt + 1) * P)
                 nc.tensor.matmul_mx(
                     out=y[h, nt][:], lhsT=wb_w[:, rows].bitcast(FP8X4), lhsT_scale=wb_s[:, rows],
                     rhs=hq_w[:].bitcast(FP8X4), rhs_scale=hq_s[:], start=False, stop=True,
                 )
-            nc.scalar.copy(y_sb[:, 0, :], y[h, 0][:])
+            cols = slice(h * HALF, (h + 1) * HALF)
             if h == 0:
-                nc.scalar.copy(y_sb[:, 1, :], y[h, 1][:])
+                y_sb = sb("y_sb0", [P, 2, HALF], F32)
+                for nt in range(2):
+                    nc.scalar.copy(y_sb[:, nt, :], y[h, nt][:])
+                nc.sync.dma_start(out.rearrange("(nt p) o -> p nt o", p=P)[:, :, cols], y_sb[:])
             else:
-                nc.vector.tensor_copy(y_sb[:, 1, :], y[h, 1][:])
-            nc.sync.dma_start(out_v[:, :, h * HALF : (h + 1) * HALF], y_sb[:])
+                y_lo = sb("y_lo", [P, HALF], F32)
+                y_hi = sb("y_hi", [P, HALF], F32)
+                nc.vector.tensor_copy(y_lo[:], y[h, 0][:])
+                nc.sync.dma_start(out[0:P, cols], y_lo[:])
+                nc.scalar.copy(y_hi[:], y[h, 1][:])
+                nc.scalar.dma_start(out[P : 2 * P, cols], y_hi[:])

@@ -57,35 +57,37 @@ def tile_picked_tokens_plain_bank_trailingbest_further_plain_kernel(
             engine.memset(t[:].bitcast(I32), 0)
             return t
 
-        def load_scales(queue, t, src):
-            for q in range(4):
+        def load_scales(queue, t, src, quadrants=range(4)):
+            for q in quadrants:
                 queue.dma_start(t[32 * q : 32 * q + 4, :].bitcast(I32), src[0, 4 * q : 4 * q + 4, :].bitcast(I32))
 
         def half(lst, h):
             return lst[:, h * LIST_COLS : (h + 1) * LIST_COLS]
 
         xt_s = cleared_scales("xt_s", xt_scales)
+        stage = shared.tile([P // 2, 2 * 2 * R], U8, name="stage", offset=0, align_bytes=64)
+        nc.vector.memset(stage[:].bitcast(I32), 0)
+
+        def load_stage(queue, which, src):
+            rows = src[0].bitcast(I32).rearrange("(u v i) c -> v i u c", u=2, v=2)
+            for v in range(2):
+                dst = stage[32 * v : 32 * v + 4, :].bitcast(I32).rearrange("i (u w c) -> i u w c", u=2, w=2)
+                queue.dma_start(dst[:, :, which, :], rows[v])
+
+        xo_w = load_e2m1("xo_w", xo_words, nc.gpsimd)
         w2_w = load_e4m3("w2_w", w2_words, nc.gpsimd)
         w_w = load_e2m1("w_w", w_words, nc.gpsimd)
         xo_s = cleared_scales("xo_s", xo_scales, nc.vector)
-        stage = shared.tile([4, 4 * 2 * R], U8, name="stage", offset=0, align_bytes=64)
         both_s = sb("both_s", [P, 2 * R], U8)
-        nc.gpsimd.memset(both_s[:].bitcast(I32), 0)
-
-        def load_stage(which, src):
-            nc.sync.dma_start(
-                stage[:].bitcast(I32).rearrange("i (q w c) -> i q w c", q=4, w=2)[:, :, which, :],
-                src[0].bitcast(I32).rearrange("(q i) c -> i q c", q=4),
-            )
 
         l1 = load_list("l1", offs)
         load_scales(nc.sync, xt_s, xt_scales)
         l2 = load_list("l2", offs2)
+        load_scales(nc.sync, xo_s, xo_scales, range(0, 1))
         xt_w = load_e4m3("xt_w", xt_words)
-        xo_w = load_e2m1("xo_w", xo_words)
-        load_scales(nc.sync, xo_s, xo_scales)
-        load_stage(0, w_scales)
-        load_stage(1, w2_scales)
+        load_scales(nc.sync, xo_s, xo_scales, range(1, 4))
+        load_stage(nc.sync, 0, w_scales)
+        load_stage(nc.sync, 1, w2_scales)
         l3 = load_list("l3", offs3)
 
         boards = [sb(f"board{b}", [P, C], F32) for b in range(BOARDS)]
@@ -127,10 +129,15 @@ def tile_picked_tokens_plain_bank_trailingbest_further_plain_kernel(
             return [dealt[:, t * P : (t + 1) * P] for t in range(PACK)]
 
         w2d_w = deal_words("w2d_w", w2_w, U32)
-        wd_w = deal_words("wd_w", w_w, U16)
+        w_by_t = w_w[:].rearrange("p (m t) -> p m t", t=PACK)
+        w_first = sb("w_first", [P, P], U16)
+        w_rest = sb("w_rest", [P, (PACK - 1) * P], U16)
+        nc.scalar.copy(w_first[:], w_by_t[:, :, 0])
+        nc.scalar.copy(w_rest[:].rearrange("p (t m) -> p m t", t=PACK - 1), w_by_t[:, :, 1:PACK])
+        wd_w = [w_first[:]] + [w_rest[:, (t - 1) * P : t * P] for t in range(1, PACK)]
 
-        for q in range(4):
-            nc.vector.tensor_copy(both_s[32 * q : 32 * q + 4, :].bitcast(I32), stage[:, 2 * R * q : 2 * R * (q + 1)].bitcast(I32))
+        for u in range(2):
+            nc.vector.tensor_copy(both_s[64 * u : 64 * u + 64, :].bitcast(I32), stage[:, 2 * R * u : 2 * R * (u + 1)].bitcast(I32))
         first_s = sb("first_s", [P, 2, P], U8)
         rest_s = sb("rest_s", [P, 2, PACK - 1, P], U8)
         both_by_t = both_s[:].rearrange("p (w m t) -> p w t m", w=2, t=PACK)
@@ -138,7 +145,8 @@ def tile_picked_tokens_plain_bank_trailingbest_further_plain_kernel(
         xg_w[1] = gather("xg_w1", xt_w, half(l1, 1), HALF, U32, at=0)
         og_w[1] = gather("og_w1", xo_w, half(l2, 1), HALF, U16, at=1024)
         og_s[1] = gather("og_s1", xo_s, half(l2, 1), HALF, U8, at=1536)
-        nc.vector.tensor_copy(rest_s[:], both_by_t[:, :, 1:PACK, :])
+        nc.gpsimd.tensor_copy(rest_s[:, :, 0, :], both_by_t[:, :, 1, :])
+        nc.gpsimd.tensor_copy(rest_s[:, :, 1:3, :], both_by_t[:, :, 2:PACK, :])
         wd_s = [first_s[:, 0, :]] + [rest_s[:, 0, t - 1, :] for t in range(1, PACK)]
         w2d_s = [first_s[:, 1, :]] + [rest_s[:, 1, t - 1, :] for t in range(1, PACK)]
 
@@ -160,11 +168,15 @@ def tile_picked_tokens_plain_bank_trailingbest_further_plain_kernel(
         nc.scalar.copy(a0_sb[0][:], acc0[0][:])
         first_product(acc0[1][:], 0, 1)
         nc.vector.tensor_copy(a0_sb[1][:], acc0[1][:])
-        for t in range(1, PACK):
+        for t in range(1, PACK - 1):
             first_product(acc[t][:, 0:HALF], t, 0)
             first_product(acc[t][:, HALF:J], t, 1)
+        last_hi = psum.tile([P, HALF], F32, name="last_hi", tag="bank1")
+        first_product(acc[3][:, 0:HALF], 3, 0)
+        first_product(last_hi[:], 3, 1)
         nc.vector.tensor_copy(a_sb[1][:], acc[1][:])
         nc.vector.tensor_copy(a_sb[2][:], acc[2][:])
+        nc.vector.tensor_copy(a_sb[3][:, 0:HALF], acc[3][:, 0:HALF])
 
         x5_s = gather("x5_s", xt_s, l5[:], O, U8)
         y = {}
@@ -187,7 +199,7 @@ def tile_picked_tokens_plain_bank_trailingbest_further_plain_kernel(
                     nc.scalar.activation(pw[:].indirect(half(l3, h)), a0_sb[h][:], COPY)
             else:
                 if t > 2:
-                    nc.scalar.copy(a_sb[t][:], acc[t][:])
+                    nc.scalar.copy(a_sb[t][:, HALF:J], last_hi[:])
                 nc.scalar.activation(pw[:].indirect(l3[:]), a_sb[t][:], COPY)
             nc.vector.tensor_tensor(g1[:, PAD + 1 : PAD + mid], pw[:, 1:mid], pw[:, 0 : mid - 1], ALU.max)
             nc.vector.tensor_scalar_max(g1[:, PAD : PAD + 1], pw[:, 0:1], 0.0)

@@ -18,10 +18,20 @@ COPY = mybir.ActivationFunctionType.Copy
 
 P = 128
 PACK = 4
+LAST = PACK - 1
 HALF = 256
-LIST_COLS = HALF // 16
+HALF_COLS = HALF // 16
+MID = C // 2
 PAD = 4
 BOARDS = 3
+ALIGN = 64
+
+AT_STAGE = 0
+AT_XG_W = AT_STAGE
+AT_OG_W = AT_XG_W + 4 * HALF
+AT_OG_S = AT_OG_W + 2 * HALF
+AT_G3 = 4096
+AT_X5_W = AT_G3 + 4 * C - 4 * O
 
 
 def tile_picked_tokens_plain_bank_trailingbest_further_plain_kernel(
@@ -31,126 +41,125 @@ def tile_picked_tokens_plain_bank_trailingbest_further_plain_kernel(
     nc = tc.nc
     with ExitStack() as ctx:
         keep = ctx.enter_context(tc.tile_pool(name="keep", bufs=1))
-        shared = ctx.enter_context(tc.tile_pool(name="shared", bufs=1))
+        reused = ctx.enter_context(tc.tile_pool(name="reused", bufs=1))
         psum = ctx.enter_context(tc.psum_pool(name="psum", bufs=1))
 
         def sb(name, shape, dtype):
-            return keep.tile(shape, dtype, name=name, align_bytes=64)
+            return keep.tile(shape, dtype, name=name, align_bytes=ALIGN)
+
+        def sb_at(name, shape, dtype, at):
+            return reused.tile(shape, dtype, name=name, offset=at, align_bytes=ALIGN)
 
         def load_list(name, src):
-            t = keep.tile([P, J // 16], U16, name=name)
-            nc.sync.dma_start(t[:], src)
-            return t
-
-        def load_e4m3(name, src, queue=nc.sync):
-            t = sb(name, [P, src.shape[2]], U32)
-            queue.dma_start(t[:].bitcast(I32), src[0].rearrange("p n t -> p (n t)").bitcast(I32))
-            return t
-
-        def load_e2m1(name, src, queue=nc.sync):
-            t = sb(name, [P, src.shape[2] // 2], U16)
-            queue.dma_start(t[:].bitcast(I32), src[0].bitcast(I32))
-            return t
-
-        def cleared_scales(name, src, engine=nc.gpsimd):
-            t = sb(name, [P, src.shape[2]], U8)
-            engine.memset(t[:].bitcast(I32), 0)
-            return t
-
-        def load_scales(queue, t, src, quadrants=range(4)):
-            for q in quadrants:
-                queue.dma_start(t[32 * q : 32 * q + 4, :].bitcast(I32), src[0, 4 * q : 4 * q + 4, :].bitcast(I32))
+            lst = keep.tile([P, J // 16], U16, name=name)
+            nc.sync.dma_start(lst[:], src)
+            return lst
 
         def half(lst, h):
-            return lst[:, h * LIST_COLS : (h + 1) * LIST_COLS]
+            return lst[:, h * HALF_COLS : (h + 1) * HALF_COLS]
 
-        xt_s = cleared_scales("xt_s", xt_scales)
-        stage = shared.tile([P // 2, 2 * 2 * R], U8, name="stage", offset=0, align_bytes=64)
+        def load_e4m3(queue, name, src):
+            words = sb(name, [P, src.shape[2]], U32)
+            queue.dma_start(words[:].bitcast(I32), src[0].rearrange("p n t -> p (n t)").bitcast(I32))
+            return words
+
+        def load_e2m1(queue, name, src):
+            words = sb(name, [P, src.shape[2] // 2], U16)
+            queue.dma_start(words[:].bitcast(I32), src[0].bitcast(I32))
+            return words
+
+        def cleared_scales(engine, name, src):
+            scales = sb(name, [P, src.shape[2]], U8)
+            engine.memset(scales[:].bitcast(I32), 0)
+            return scales
+
+        def load_scales(scales, src):
+            for q in range(4):
+                nc.sync.dma_start(scales[32 * q : 32 * q + 4, :].bitcast(I32), src[0, 4 * q : 4 * q + 4, :].bitcast(I32))
+
+        def gather(dst, window, offsets):
+            nc.vector.tensor_copy(dst[:], window[:].indirect(offsets))
+            return dst
+
+        xt_s = cleared_scales(nc.gpsimd, "xt_s", xt_scales)
+        xo_s = cleared_scales(nc.vector, "xo_s", xo_scales)
+
+        stage = sb_at("stage", [P // 2, 2 * 2 * R], U8, AT_STAGE)
         nc.vector.memset(stage[:].bitcast(I32), 0)
 
-        def load_stage(queue, which, src):
+        def load_stage(which, src):
             rows = src[0].bitcast(I32).rearrange("(u v i) c -> v i u c", u=2, v=2)
             for v in range(2):
                 dst = stage[32 * v : 32 * v + 4, :].bitcast(I32).rearrange("i (u w c) -> i u w c", u=2, w=2)
-                queue.dma_start(dst[:, :, which, :], rows[v])
+                nc.sync.dma_start(dst[:, :, which, :], rows[v])
 
-        xo_w = load_e2m1("xo_w", xo_words, nc.gpsimd)
-        w2_w = load_e4m3("w2_w", w2_words, nc.gpsimd)
-        w_w = load_e2m1("w_w", w_words, nc.gpsimd)
-        xo_s = cleared_scales("xo_s", xo_scales, nc.vector)
-        both_s = sb("both_s", [P, 2 * R], U8)
+        xo_w = load_e2m1(nc.gpsimd, "xo_w", xo_words)
+        w2_w = load_e4m3(nc.gpsimd, "w2_w", w2_words)
+        w_w = load_e2m1(nc.gpsimd, "w_w", w_words)
 
-        l1 = load_list("l1", offs)
-        load_scales(nc.sync, xt_s, xt_scales)
-        l2 = load_list("l2", offs2)
-        load_scales(nc.sync, xo_s, xo_scales, range(0, 1))
-        xt_w = load_e4m3("xt_w", xt_words)
-        load_scales(nc.sync, xo_s, xo_scales, range(1, 4))
-        load_stage(nc.sync, 0, w_scales)
-        load_stage(nc.sync, 1, w2_scales)
-        l3 = load_list("l3", offs3)
+        list1 = load_list("list1", offs)
+        load_scales(xt_s, xt_scales)
+        xt_w = load_e4m3(nc.sync, "xt_w", xt_words)
+        list2 = load_list("list2", offs2)
+        load_scales(xo_s, xo_scales)
+        load_stage(0, w_scales)
+        load_stage(1, w2_scales)
+        list3 = load_list("list3", offs3)
 
         boards = [sb(f"board{b}", [P, C], F32) for b in range(BOARDS)]
         nc.vector.memset(boards[0][:], 0.0)
         nc.gpsimd.memset(boards[1][:], 0.0)
         g1 = sb("g1", [P, PAD + C], F32)
         nc.vector.memset(g1[:, 0:PAD], 0.0)
-        wb_s = cleared_scales("wb_s", wb_scales)
-        ws_s = cleared_scales("ws_s", ws_scales)
+        wb_s = cleared_scales(nc.gpsimd, "wb_s", wb_scales)
+        ws_s = cleared_scales(nc.gpsimd, "ws_s", ws_scales)
         nc.gpsimd.memset(boards[2][:], 0.0)
 
-        l5 = load_list("l5", offs5)
-        l4 = load_list("l4", offs4)
+        list5 = load_list("list5", offs5)
+        list4 = load_list("list4", offs4)
         sa_t = sb("sa_t", [P, PACK], F32)
         nc.sync.dma_start(sa_t[:], sa.rearrange("(p t) o -> p (t o)", t=PACK))
-        ws_w = load_e2m1("ws_w", ws_words)
-        load_scales(nc.sync, ws_s, ws_scales)
-        wb_w = load_e4m3("wb_w", wb_words)
-        load_scales(nc.sync, wb_s, wb_scales)
+        ws_w = load_e2m1(nc.sync, "ws_w", ws_words)
+        load_scales(ws_s, ws_scales)
+        wb_w = load_e4m3(nc.sync, "wb_w", wb_words)
+        load_scales(wb_s, wb_scales)
 
-        def gather(name, window, offsets, n, dtype, at=None):
-            if at is None:
-                t = sb(name, [P, n], dtype)
-            else:
-                t = shared.tile([P, n], dtype, name=name, offset=at, align_bytes=64)
-            nc.vector.tensor_copy(t[:], window[:].indirect(offsets))
-            return t
+        xg_s = [gather(sb("xg_s0", [P, HALF], U8), xt_s, half(list1, 0))]
+        xg_w = [gather(sb("xg_w0", [P, HALF], U32), xt_w, half(list1, 0))]
+        og_w = [gather(sb("og_w0", [P, HALF], U16), xo_w, half(list2, 0))]
+        og_s = [gather(sb("og_s0", [P, HALF], U8), xo_s, half(list2, 0))]
+        xg_s.append(gather(sb("xg_s1", [P, HALF], U8), xt_s, half(list1, 1)))
 
-        xg_s, xg_w, og_s, og_w = [None, None], [None, None], [None, None], [None, None]
-        xg_s[0] = gather("xg_s0", xt_s, half(l1, 0), HALF, U8)
-        xg_w[0] = gather("xg_w0", xt_w, half(l1, 0), HALF, U32)
-        og_w[0] = gather("og_w0", xo_w, half(l2, 0), HALF, U16)
-        og_s[0] = gather("og_s0", xo_s, half(l2, 0), HALF, U8)
-        xg_s[1] = gather("xg_s1", xt_s, half(l1, 1), HALF, U8)
-
-        def deal_words(name, src, dtype):
-            dealt = sb(name, [P, R], dtype)
-            nc.scalar.copy(dealt[:].rearrange("p (t m) -> p m t", t=PACK), src[:].rearrange("p (m t) -> p m t", t=PACK))
-            return [dealt[:, t * P : (t + 1) * P] for t in range(PACK)]
-
-        w2d_w = deal_words("w2d_w", w2_w, U32)
+        w2_dealt = sb("w2_dealt", [P, R], U32)
+        nc.scalar.copy(w2_dealt[:].rearrange("p (t m) -> p m t", t=PACK), w2_w[:].rearrange("p (m t) -> p m t", t=PACK))
+        w2d_w = [w2_dealt[:, t * P : (t + 1) * P] for t in range(PACK)]
         w_by_t = w_w[:].rearrange("p (m t) -> p m t", t=PACK)
         w_first = sb("w_first", [P, P], U16)
-        w_rest = sb("w_rest", [P, (PACK - 1) * P], U16)
+        w_rest = sb("w_rest", [P, LAST * P], U16)
         nc.scalar.copy(w_first[:], w_by_t[:, :, 0])
-        nc.scalar.copy(w_rest[:].rearrange("p (t m) -> p m t", t=PACK - 1), w_by_t[:, :, 1:PACK])
+        nc.scalar.copy(w_rest[:].rearrange("p (t m) -> p m t", t=LAST), w_by_t[:, :, 1:PACK])
         wd_w = [w_first[:]] + [w_rest[:, (t - 1) * P : t * P] for t in range(1, PACK)]
 
+        both_s = sb("both_s", [P, 2 * R], U8)
         for u in range(2):
-            nc.vector.tensor_copy(both_s[64 * u : 64 * u + 64, :].bitcast(I32), stage[:, 2 * R * u : 2 * R * (u + 1)].bitcast(I32))
+            nc.vector.tensor_copy(
+                both_s[64 * u : 64 * u + 64, :].bitcast(I32), stage[:, 2 * R * u : 2 * R * (u + 1)].bitcast(I32)
+            )
         first_s = sb("first_s", [P, 2, P], U8)
-        rest_s = sb("rest_s", [P, 2, PACK - 1, P], U8)
+        rest_s = sb("rest_s", [P, 2, LAST, P], U8)
         both_by_t = both_s[:].rearrange("p (w m t) -> p w t m", w=2, t=PACK)
         nc.vector.tensor_copy(first_s[:], both_by_t[:, :, 0, :])
-        xg_w[1] = gather("xg_w1", xt_w, half(l1, 1), HALF, U32, at=0)
-        og_w[1] = gather("og_w1", xo_w, half(l2, 1), HALF, U16, at=1024)
-        og_s[1] = gather("og_s1", xo_s, half(l2, 1), HALF, U8, at=1536)
+
+        xg_w.append(gather(sb_at("xg_w1", [P, HALF], U32, AT_XG_W), xt_w, half(list1, 1)))
+        og_w.append(gather(sb_at("og_w1", [P, HALF], U16, AT_OG_W), xo_w, half(list2, 1)))
+        og_s.append(gather(sb_at("og_s1", [P, HALF], U8, AT_OG_S), xo_s, half(list2, 1)))
+
         nc.gpsimd.tensor_copy(rest_s[:, :, 0, :], both_by_t[:, :, 1, :])
-        nc.gpsimd.tensor_copy(rest_s[:, :, 1:3, :], both_by_t[:, :, 2:PACK, :])
+        nc.gpsimd.tensor_copy(rest_s[:, :, 1:LAST, :], both_by_t[:, :, 2:PACK, :])
         wd_s = [first_s[:, 0, :]] + [rest_s[:, 0, t - 1, :] for t in range(1, PACK)]
         w2d_s = [first_s[:, 1, :]] + [rest_s[:, 1, t - 1, :] for t in range(1, PACK)]
 
-        def first_product(acc, t, h):
+        def hidden_product(acc, t, h):
             nc.tensor.matmul_mx(
                 out=acc, lhsT=wd_w[t].bitcast(FP4X4), lhsT_scale=wd_s[t],
                 rhs=xg_w[h][:].bitcast(FP8X4), rhs_scale=xg_s[h][:], start=True, stop=False,
@@ -162,99 +171,96 @@ def tile_picked_tokens_plain_bank_trailingbest_further_plain_kernel(
 
         acc0 = [psum.tile([P, HALF], F32, name=f"acc0{h}", tag=f"bank{h}") for h in range(2)]
         a0_sb = [sb(f"a0{h}", [P, HALF], F32) for h in range(2)]
-        acc = [None] + [psum.tile([P, J], F32, name=f"acc{t}", tag=f"bank{t + 1}") for t in range(1, PACK)]
-        a_sb = [None] + [sb(f"a{t}", [P, J], F32) for t in range(1, PACK)]
-        first_product(acc0[0][:], 0, 0)
+        acc = {t: psum.tile([P, J], F32, name=f"acc{t}", tag=f"bank{t + 1}") for t in range(1, PACK)}
+        a_sb = {t: sb(f"a{t}", [P, J], F32) for t in range(1, PACK)}
+        hidden_product(acc0[0][:], 0, 0)
         nc.scalar.copy(a0_sb[0][:], acc0[0][:])
-        first_product(acc0[1][:], 0, 1)
+        hidden_product(acc0[1][:], 0, 1)
         nc.vector.tensor_copy(a0_sb[1][:], acc0[1][:])
-        for t in range(1, PACK - 1):
-            first_product(acc[t][:, 0:HALF], t, 0)
-            first_product(acc[t][:, HALF:J], t, 1)
-        last_hi = psum.tile([P, HALF], F32, name="last_hi", tag="bank1")
-        first_product(acc[3][:, 0:HALF], 3, 0)
-        first_product(last_hi[:], 3, 1)
-        nc.vector.tensor_copy(a_sb[1][:], acc[1][:])
-        nc.vector.tensor_copy(a_sb[2][:], acc[2][:])
-        nc.vector.tensor_copy(a_sb[3][:, 0:HALF], acc[3][:, 0:HALF])
+        for t in range(1, LAST):
+            hidden_product(acc[t][:, 0:HALF], t, 0)
+            hidden_product(acc[t][:, HALF:J], t, 1)
+        acc_last_hi = psum.tile([P, HALF], F32, name="acc_last_hi", tag="bank1")
+        hidden_product(acc[LAST][:, 0:HALF], LAST, 0)
+        hidden_product(acc_last_hi[:], LAST, 1)
+        for t in range(1, LAST):
+            nc.vector.tensor_copy(a_sb[t][:], acc[t][:])
+        nc.vector.tensor_copy(a_sb[LAST][:, 0:HALF], acc[LAST][:, 0:HALF])
 
-        x5_s = gather("x5_s", xt_s, l5[:], O, U8)
-        y = {}
+        x5_s = gather(sb("x5_s", [P, O], U8), xt_s, list5[:])
 
-        def short_way(h):
-            for nt in range(2):
-                rows = slice(nt * P, (nt + 1) * P)
-                y[h, nt] = psum.tile([P, HALF], F32, name=f"y{h}{nt}", tag=f"bank{(5 + 2 * h + nt) % 8}")
-                nc.tensor.matmul_mx(
-                    out=y[h, nt][:], lhsT=ws_w[:, rows].bitcast(FP4X4), lhsT_scale=ws_s[:, rows],
-                    rhs=x5_w[:, h * HALF : (h + 1) * HALF].bitcast(FP8X4), rhs_scale=x5_s[:, h * HALF : (h + 1) * HALF], start=True, stop=False,
-                )
-        g3 = shared.tile([P, C], F32, name="g3", offset=4096, align_bytes=64)
+        g3 = sb_at("g3", [P, C], F32, AT_G3)
         pg = [sb(f"pg{t}", [P, C], F32) for t in range(PACK)]
-        mid = C // 2
         for t in range(PACK):
             pw = boards[t % BOARDS]
             if t == 0:
                 for h in range(2):
-                    nc.scalar.activation(pw[:].indirect(half(l3, h)), a0_sb[h][:], COPY)
+                    nc.scalar.activation(pw[:].indirect(half(list3, h)), a0_sb[h][:], COPY)
             else:
-                if t > 2:
-                    nc.scalar.copy(a_sb[t][:, HALF:J], last_hi[:])
-                nc.scalar.activation(pw[:].indirect(l3[:]), a_sb[t][:], COPY)
-            nc.vector.tensor_tensor(g1[:, PAD + 1 : PAD + mid], pw[:, 1:mid], pw[:, 0 : mid - 1], ALU.max)
+                if t == LAST:
+                    nc.scalar.copy(a_sb[t][:, HALF:J], acc_last_hi[:])
+                nc.scalar.activation(pw[:].indirect(list3[:]), a_sb[t][:], COPY)
+            nc.vector.tensor_tensor(g1[:, PAD + 1 : PAD + MID], pw[:, 1:MID], pw[:, 0 : MID - 1], ALU.max)
             nc.vector.tensor_scalar_max(g1[:, PAD : PAD + 1], pw[:, 0:1], 0.0)
-            nc.vector.tensor_tensor(g1[:, PAD + mid : PAD + C], pw[:, mid:C], pw[:, mid - 1 : C - 1], ALU.max)
-            for lo in (0, mid):
+            nc.vector.tensor_tensor(g1[:, PAD + MID : PAD + C], pw[:, MID:C], pw[:, MID - 1 : C - 1], ALU.max)
+            for lo in (0, MID):
                 nc.vector.tensor_tensor(
-                    g3[:, lo : lo + mid], g1[:, PAD + lo : PAD + lo + mid],
-                    g1[:, PAD + lo - 2 : PAD + lo - 2 + mid], ALU.max,
+                    g3[:, lo : lo + MID], g1[:, PAD + lo : PAD + lo + MID],
+                    g1[:, PAD + lo - 2 : PAD + lo - 2 + MID], ALU.max,
                 )
-            for lo in (0, mid):
-                nc.vector.tensor_tensor(pg[t][:, lo : lo + mid], g3[:, lo : lo + mid], pw[:, lo : lo + mid], ALU.subtract)
+            for lo in (0, MID):
+                nc.vector.tensor_tensor(pg[t][:, lo : lo + MID], g3[:, lo : lo + MID], pw[:, lo : lo + MID], ALU.subtract)
 
-        x5_w = gather("x5_w", xt_w, l5[:], O, U32, at=4096 + 4 * C - 4 * O)
-        short_way(0)
-        short_way(1)
+        x5_w = gather(sb_at("x5_w", [P, O], U32, AT_X5_W), xt_w, list5[:])
+        y = {}
+        for h in range(2):
+            places = slice(h * HALF, (h + 1) * HALF)
+            for nt in range(2):
+                features = slice(nt * P, (nt + 1) * P)
+                y[h, nt] = psum.tile([P, HALF], F32, name=f"y{h}{nt}", tag=f"bank{(5 + 2 * h + nt) % 8}")
+                nc.tensor.matmul_mx(
+                    out=y[h, nt][:], lhsT=ws_w[:, features].bitcast(FP4X4), lhsT_scale=ws_s[:, features],
+                    rhs=x5_w[:, places].bitcast(FP8X4), rhs_scale=x5_s[:, places], start=True, stop=False,
+                )
 
         hid = [sb(f"hid{h}", [P, PACK, HALF], BF16) for h in range(2)]
         for t in range(PACK):
             for h in range(2):
-                nc.scalar.activation(hid[h][:, t, :], pg[t][:].indirect(half(l4, h)), COPY, scale=sa_t[:, t : t + 1])
+                nc.scalar.activation(hid[h][:, t, :], pg[t][:].indirect(half(list4, h)), COPY, scale=sa_t[:, t : t + 1])
 
         woven = [sb(f"woven{h}", [P, HALF * PACK], BF16) for h in range(2)]
-
-        def weave(h, lo, hi):
+        quarter = HALF // 2
+        for h, width in ((0, HALF), (1, quarter)):
             nc.vector.tensor_copy(
-                woven[h][:, PACK * lo : PACK * hi].rearrange("p (c i t) -> p c t i", i=4, t=PACK),
-                hid[h][:, :, lo:hi].rearrange("p t (c i) -> p c t i", i=4),
+                woven[h][:, 0 : PACK * width].rearrange("p (c i t) -> p c t i", i=4, t=PACK),
+                hid[h][:, :, 0:width].rearrange("p t (c i) -> p c t i", i=4),
             )
-
-        weave(0, 0, HALF)
-        weave(1, 0, P)
         nc.scalar.copy(
-            woven[1][:, PACK * P : PACK * HALF].rearrange("p (c t) -> p c t", t=PACK),
-            hid[1][:, :, P:HALF].rearrange("p t c -> p c t"),
+            woven[1][:, PACK * quarter : PACK * HALF].rearrange("p (c t) -> p c t", t=PACK),
+            hid[1][:, :, quarter:HALF].rearrange("p t c -> p c t"),
         )
-        for h in range(2):
+
+        def output_product(h):
             hq_w = sb(f"hq_w{h}", [P, HALF], U32)
             hq_s = sb(f"hq_s{h}", [P, HALF], U8)
             nc.vector.quantize_mx(out=hq_w[:].bitcast(FP8X4), scales=hq_s[:], in_=woven[h][:])
             for nt in range(2):
-                rows = slice(nt * P, (nt + 1) * P)
+                features = slice(nt * P, (nt + 1) * P)
                 nc.tensor.matmul_mx(
-                    out=y[h, nt][:], lhsT=wb_w[:, rows].bitcast(FP8X4), lhsT_scale=wb_s[:, rows],
+                    out=y[h, nt][:], lhsT=wb_w[:, features].bitcast(FP8X4), lhsT_scale=wb_s[:, features],
                     rhs=hq_w[:].bitcast(FP8X4), rhs_scale=hq_s[:], start=False, stop=True,
                 )
-            cols = slice(h * HALF, (h + 1) * HALF)
-            if h == 0:
-                y_sb = sb("y_sb0", [P, 2, HALF], F32)
-                for nt in range(2):
-                    nc.scalar.copy(y_sb[:, nt, :], y[h, nt][:])
-                nc.sync.dma_start(out.rearrange("(nt p) o -> p nt o", p=P)[:, :, cols], y_sb[:])
-            else:
-                y_lo = sb("y_lo", [P, HALF], F32)
-                y_hi = sb("y_hi", [P, HALF], F32)
-                nc.vector.tensor_copy(y_lo[:], y[h, 0][:])
-                nc.sync.dma_start(out[0:P, cols], y_lo[:])
-                nc.scalar.copy(y_hi[:], y[h, 1][:])
-                nc.scalar.dma_start(out[P : 2 * P, cols], y_hi[:])
+
+        output_product(0)
+        y_first = sb("y_first", [P, 2, HALF], F32)
+        for nt in range(2):
+            nc.scalar.copy(y_first[:, nt, :], y[0, nt][:])
+        nc.sync.dma_start(out.rearrange("(nt p) o -> p nt o", p=P)[:, :, 0:HALF], y_first[:])
+
+        output_product(1)
+        y_lo = sb("y_lo", [P, HALF], F32)
+        y_hi = sb("y_hi", [P, HALF], F32)
+        nc.vector.tensor_copy(y_lo[:], y[1, 0][:])
+        nc.sync.dma_start(out[0:P, HALF:O], y_lo[:])
+        nc.scalar.copy(y_hi[:], y[1, 1][:])
+        nc.scalar.dma_start(out[P : 2 * P, HALF:O], y_hi[:])

from contextlib import ExitStack

import concourse.mybir as mybir

K, J, R, T, Z, M, C, O, N = 512, 512, 512, 1024, 512, 1024, 1024, 512, 256
FLOPS = 2 * (K * R * J + Z * R * J + R * N * O + K * N * O)

F32 = mybir.dt.float32
BF16 = mybir.dt.bfloat16
I32 = mybir.dt.int32
U32 = mybir.dt.uint32
U16 = mybir.dt.uint16
U8 = mybir.dt.uint8
FP8X4 = mybir.dt.float8_e4m3fn_x4
FP4X4 = mybir.dt.float4_e2m1fn_x4
ALU = mybir.AluOpType
COPY = mybir.ActivationFunctionType.Copy

P = 128
PACK = 4
LAST = PACK - 1
HALF = 256
HALF_COLS = HALF // 16
MID = C // 2
PAD = 4
BOARDS = 3
ALIGN = 64

AT_STAGE = 0
AT_XG_W = AT_STAGE
AT_OG_W = AT_XG_W + 4 * HALF
AT_OG_S = AT_OG_W + 2 * HALF
AT_G3 = 4096
AT_X5_W = AT_G3 + 4 * C - 4 * O


def tile_picked_tokens_plain_bank_trailingbest_further_plain_kernel(
    tc, xt_words, xt_scales, w_words, w_scales, xo_words, xo_scales, w2_words, w2_scales, sa,
    wb_words, wb_scales, ws_words, ws_scales, offs, offs2, offs3, offs4, offs5, out,
):
    nc = tc.nc
    with ExitStack() as ctx:
        keep = ctx.enter_context(tc.tile_pool(name="keep", bufs=1))
        reused = ctx.enter_context(tc.tile_pool(name="reused", bufs=1))
        psum = ctx.enter_context(tc.psum_pool(name="psum", bufs=1))

        def sb(name, shape, dtype):
            return keep.tile(shape, dtype, name=name, align_bytes=ALIGN)

        def sb_at(name, shape, dtype, at):
            return reused.tile(shape, dtype, name=name, offset=at, align_bytes=ALIGN)

        def load_list(name, src):
            lst = keep.tile([P, J // 16], U16, name=name)
            nc.sync.dma_start(lst[:], src)
            return lst

        def half(lst, h):
            return lst[:, h * HALF_COLS : (h + 1) * HALF_COLS]

        def load_e4m3(queue, name, src):
            words = sb(name, [P, src.shape[2]], U32)
            queue.dma_start(words[:].bitcast(I32), src[0].rearrange("p n t -> p (n t)").bitcast(I32))
            return words

        def load_e2m1(queue, name, src):
            words = sb(name, [P, src.shape[2] // 2], U16)
            queue.dma_start(words[:].bitcast(I32), src[0].bitcast(I32))
            return words

        def cleared_scales(engine, name, src):
            scales = sb(name, [P, src.shape[2]], U8)
            engine.memset(scales[:].bitcast(I32), 0)
            return scales

        def load_scales(scales, src):
            for q in range(4):
                nc.sync.dma_start(scales[32 * q : 32 * q + 4, :].bitcast(I32), src[0, 4 * q : 4 * q + 4, :].bitcast(I32))

        def gather(dst, window, offsets):
            nc.vector.tensor_copy(dst[:], window[:].indirect(offsets))
            return dst

        xt_s = cleared_scales(nc.gpsimd, "xt_s", xt_scales)
        xo_s = cleared_scales(nc.vector, "xo_s", xo_scales)

        stage = sb_at("stage", [P // 2, 2 * 2 * R], U8, AT_STAGE)
        nc.vector.memset(stage[:].bitcast(I32), 0)

        def load_stage(which, src):
            rows = src[0].bitcast(I32).rearrange("(u v i) c -> v i u c", u=2, v=2)
            for v in range(2):
                dst = stage[32 * v : 32 * v + 4, :].bitcast(I32).rearrange("i (u w c) -> i u w c", u=2, w=2)
                nc.sync.dma_start(dst[:, :, which, :], rows[v])

        xo_w = load_e2m1(nc.gpsimd, "xo_w", xo_words)
        w2_w = load_e4m3(nc.gpsimd, "w2_w", w2_words)
        w_w = load_e2m1(nc.gpsimd, "w_w", w_words)

        list1 = load_list("list1", offs)
        load_scales(xt_s, xt_scales)
        xt_w = load_e4m3(nc.sync, "xt_w", xt_words)
        list2 = load_list("list2", offs2)
        load_scales(xo_s, xo_scales)
        load_stage(0, w_scales)
        load_stage(1, w2_scales)
        list3 = load_list("list3", offs3)

        boards = [sb(f"board{b}", [P, C], F32) for b in range(BOARDS)]
        nc.vector.memset(boards[0][:], 0.0)
        nc.gpsimd.memset(boards[1][:], 0.0)
        g1 = sb("g1", [P, PAD + C], F32)
        nc.vector.memset(g1[:, 0:PAD], 0.0)
        wb_s = cleared_scales(nc.gpsimd, "wb_s", wb_scales)
        ws_s = cleared_scales(nc.gpsimd, "ws_s", ws_scales)
        nc.gpsimd.memset(boards[2][:], 0.0)

        list5 = load_list("list5", offs5)
        list4 = load_list("list4", offs4)
        sa_t = sb("sa_t", [P, PACK], F32)
        nc.sync.dma_start(sa_t[:], sa.rearrange("(p t) o -> p (t o)", t=PACK))
        ws_w = load_e2m1(nc.sync, "ws_w", ws_words)
        load_scales(ws_s, ws_scales)
        wb_w = load_e4m3(nc.sync, "wb_w", wb_words)
        load_scales(wb_s, wb_scales)

        xg_s = [gather(sb("xg_s0", [P, HALF], U8), xt_s, half(list1, 0))]
        xg_w = [gather(sb("xg_w0", [P, HALF], U32), xt_w, half(list1, 0))]
        og_w = [gather(sb("og_w0", [P, HALF], U16), xo_w, half(list2, 0))]
        og_s = [gather(sb("og_s0", [P, HALF], U8), xo_s, half(list2, 0))]
        xg_s.append(gather(sb("xg_s1", [P, HALF], U8), xt_s, half(list1, 1)))

        w2_dealt = sb("w2_dealt", [P, R], U32)
        nc.scalar.copy(w2_dealt[:].rearrange("p (t m) -> p m t", t=PACK), w2_w[:].rearrange("p (m t) -> p m t", t=PACK))
        w2d_w = [w2_dealt[:, t * P : (t + 1) * P] for t in range(PACK)]
        w_by_t = w_w[:].rearrange("p (m t) -> p m t", t=PACK)
        w_first = sb("w_first", [P, P], U16)
        w_rest = sb("w_rest", [P, LAST * P], U16)
        nc.scalar.copy(w_first[:], w_by_t[:, :, 0])
        nc.scalar.copy(w_rest[:].rearrange("p (t m) -> p m t", t=LAST), w_by_t[:, :, 1:PACK])
        wd_w = [w_first[:]] + [w_rest[:, (t - 1) * P : t * P] for t in range(1, PACK)]

        both_s = sb("both_s", [P, 2 * R], U8)
        for u in range(2):
            nc.vector.tensor_copy(
                both_s[64 * u : 64 * u + 64, :].bitcast(I32), stage[:, 2 * R * u : 2 * R * (u + 1)].bitcast(I32)
            )
        first_s = sb("first_s", [P, 2, P], U8)
        rest_s = sb("rest_s", [P, 2, LAST, P], U8)
        both_by_t = both_s[:].rearrange("p (w m t) -> p w t m", w=2, t=PACK)
        nc.vector.tensor_copy(first_s[:], both_by_t[:, :, 0, :])

        xg_w.append(gather(sb_at("xg_w1", [P, HALF], U32, AT_XG_W), xt_w, half(list1, 1)))
        og_w.append(gather(sb_at("og_w1", [P, HALF], U16, AT_OG_W), xo_w, half(list2, 1)))
        og_s.append(gather(sb_at("og_s1", [P, HALF], U8, AT_OG_S), xo_s, half(list2, 1)))

        nc.gpsimd.tensor_copy(rest_s[:, :, 0, :], both_by_t[:, :, 1, :])
        nc.gpsimd.tensor_copy(rest_s[:, :, 1:LAST, :], both_by_t[:, :, 2:PACK, :])
        wd_s = [first_s[:, 0, :]] + [rest_s[:, 0, t - 1, :] for t in range(1, PACK)]
        w2d_s = [first_s[:, 1, :]] + [rest_s[:, 1, t - 1, :] for t in range(1, PACK)]

        def hidden_product(acc, t, h):
            nc.tensor.matmul_mx(
                out=acc, lhsT=wd_w[t].bitcast(FP4X4), lhsT_scale=wd_s[t],
                rhs=xg_w[h][:].bitcast(FP8X4), rhs_scale=xg_s[h][:], start=True, stop=False,
            )
            nc.tensor.matmul_mx(
                out=acc, lhsT=w2d_w[t].bitcast(FP8X4), lhsT_scale=w2d_s[t],
                rhs=og_w[h][:].bitcast(FP4X4), rhs_scale=og_s[h][:], start=False, stop=True,
            )

        acc0 = [psum.tile([P, HALF], F32, name=f"acc0{h}", tag=f"bank{h}") for h in range(2)]
        a0_sb = [sb(f"a0{h}", [P, HALF], F32) for h in range(2)]
        acc = {t: psum.tile([P, J], F32, name=f"acc{t}", tag=f"bank{t + 1}") for t in range(1, PACK)}
        a_sb = {t: sb(f"a{t}", [P, J], F32) for t in range(1, PACK)}
        hidden_product(acc0[0][:], 0, 0)
        nc.scalar.copy(a0_sb[0][:], acc0[0][:])
        hidden_product(acc0[1][:], 0, 1)
        nc.vector.tensor_copy(a0_sb[1][:], acc0[1][:])
        for t in range(1, LAST):
            hidden_product(acc[t][:, 0:HALF], t, 0)
            hidden_product(acc[t][:, HALF:J], t, 1)
        acc_last_hi = psum.tile([P, HALF], F32, name="acc_last_hi", tag="bank1")
        hidden_product(acc[LAST][:, 0:HALF], LAST, 0)
        hidden_product(acc_last_hi[:], LAST, 1)
        for t in range(1, LAST):
            nc.vector.tensor_copy(a_sb[t][:], acc[t][:])
        nc.vector.tensor_copy(a_sb[LAST][:, 0:HALF], acc[LAST][:, 0:HALF])

        x5_s = gather(sb("x5_s", [P, O], U8), xt_s, list5[:])

        g3 = sb_at("g3", [P, C], F32, AT_G3)
        pg = [sb(f"pg{t}", [P, C], F32) for t in range(PACK)]
        for t in range(PACK):
            pw = boards[t % BOARDS]
            if t == 0:
                for h in range(2):
                    nc.scalar.activation(pw[:].indirect(half(list3, h)), a0_sb[h][:], COPY)
            else:
                if t == LAST:
                    nc.scalar.copy(a_sb[t][:, HALF:J], acc_last_hi[:])
                nc.scalar.activation(pw[:].indirect(list3[:]), a_sb[t][:], COPY)
            nc.vector.tensor_tensor(g1[:, PAD + 1 : PAD + MID], pw[:, 1:MID], pw[:, 0 : MID - 1], ALU.max)
            nc.vector.tensor_scalar_max(g1[:, PAD : PAD + 1], pw[:, 0:1], 0.0)
            nc.vector.tensor_tensor(g1[:, PAD + MID : PAD + C], pw[:, MID:C], pw[:, MID - 1 : C - 1], ALU.max)
            for lo in (0, MID):
                nc.vector.tensor_tensor(
                    g3[:, lo : lo + MID], g1[:, PAD + lo : PAD + lo + MID],
                    g1[:, PAD + lo - 2 : PAD + lo - 2 + MID], ALU.max,
                )
            for lo in (0, MID):
                nc.vector.tensor_tensor(pg[t][:, lo : lo + MID], g3[:, lo : lo + MID], pw[:, lo : lo + MID], ALU.subtract)

        x5_w = gather(sb_at("x5_w", [P, O], U32, AT_X5_W), xt_w, list5[:])
        y = {}
        for h in range(2):
            places = slice(h * HALF, (h + 1) * HALF)
            for nt in range(2):
                features = slice(nt * P, (nt + 1) * P)
                y[h, nt] = psum.tile([P, HALF], F32, name=f"y{h}{nt}", tag=f"bank{(5 + 2 * h + nt) % 8}")
                nc.tensor.matmul_mx(
                    out=y[h, nt][:], lhsT=ws_w[:, features].bitcast(FP4X4), lhsT_scale=ws_s[:, features],
                    rhs=x5_w[:, places].bitcast(FP8X4), rhs_scale=x5_s[:, places], start=True, stop=False,
                )

        hid = [sb(f"hid{h}", [P, PACK, HALF], BF16) for h in range(2)]
        for t in range(PACK):
            for h in range(2):
                nc.scalar.activation(hid[h][:, t, :], pg[t][:].indirect(half(list4, h)), COPY, scale=sa_t[:, t : t + 1])

        woven = [sb(f"woven{h}", [P, HALF * PACK], BF16) for h in range(2)]
        quarter = HALF // 2
        for h, width in ((0, HALF), (1, quarter)):
            nc.vector.tensor_copy(
                woven[h][:, 0 : PACK * width].rearrange("p (c i t) -> p c t i", i=4, t=PACK),
                hid[h][:, :, 0:width].rearrange("p t (c i) -> p c t i", i=4),
            )
        nc.scalar.copy(
            woven[1][:, PACK * quarter : PACK * HALF].rearrange("p (c t) -> p c t", t=PACK),
            hid[1][:, :, quarter:HALF].rearrange("p t c -> p c t"),
        )

        def output_product(h):
            hq_w = sb(f"hq_w{h}", [P, HALF], U32)
            hq_s = sb(f"hq_s{h}", [P, HALF], U8)
            nc.vector.quantize_mx(out=hq_w[:].bitcast(FP8X4), scales=hq_s[:], in_=woven[h][:])
            for nt in range(2):
                features = slice(nt * P, (nt + 1) * P)
                nc.tensor.matmul_mx(
                    out=y[h, nt][:], lhsT=wb_w[:, features].bitcast(FP8X4), lhsT_scale=wb_s[:, features],
                    rhs=hq_w[:].bitcast(FP8X4), rhs_scale=hq_s[:], start=False, stop=True,
                )

        output_product(0)
        y_first = sb("y_first", [P, 2, HALF], F32)
        for nt in range(2):
            nc.scalar.copy(y_first[:, nt, :], y[0, nt][:])
        nc.sync.dma_start(out.rearrange("(nt p) o -> p nt o", p=P)[:, :, 0:HALF], y_first[:])

        output_product(1)
        y_lo = sb("y_lo", [P, HALF], F32)
        y_hi = sb("y_hi", [P, HALF], F32)
        nc.vector.tensor_copy(y_lo[:], y[1, 0][:])
        nc.sync.dma_start(out[0:P, HALF:O], y_lo[:])
        nc.scalar.copy(y_hi[:], y[1, 1][:])
        nc.scalar.dma_start(out[P : 2 * P, HALF:O], y_hi[:])
